import numpy as np
import ml_dtypes


def mxq(x, axis, fmt="e4m3"):
    dtype, down = {"e4m3": (ml_dtypes.float8_e4m3fn, 7), "e5m2": (ml_dtypes.float8_e5m2, 14)}[fmt]
    v = np.moveaxis(np.asarray(x, np.float32).astype(ml_dtypes.bfloat16).astype(np.float64), axis, -1)
    blocks = v.reshape(v.shape[:-1] + (-1, 32))
    amax = np.abs(blocks).max(-1, keepdims=True)
    byte = np.maximum(np.where(amax > 0, np.frexp(amax)[1] - 1 + 127, 0) - down, 1)
    scale = np.exp2(byte - 127.0)
    codes = (blocks / scale).astype(np.float32).astype(dtype).astype(np.float64)
    return np.moveaxis((codes * scale).reshape(v.shape), -1, axis)


WIDE = False


def mx_kscale(k):
    if not WIDE:
        return np.ones(k)
    levels = np.array([10, -10, 5, -5, 0])
    if k % 512:
        return np.exp2(np.random.permutation(np.resize(levels, k // 32))).repeat(32)
    a = np.empty((k // 512, 16))
    for p in range(k // 512):
        a[p, :8] = np.random.permutation(np.resize(levels, 8))
        for g in range(8):
            far = levels[np.abs(levels - a[p, g]) >= 10]
            a[p, g + 8] = far[np.random.randint(len(far))]
    return np.exp2(a.ravel()).repeat(32)


def f64(x):
    return np.asarray(x).astype(np.float64)


def split(x):
    m, e = np.frexp(f64(x))
    hi = np.ldexp(np.trunc(16.0 * m) / 16.0, e)
    return hi, f64(x) - hi


K, M, T = 1536, 1536, 512


def setup_inputs():
    n = np.random.standard_normal
    s = mx_kscale(K)[:, None]
    return {
        "w": (n((K, M)) / np.sqrt(K) / s).astype(np.float32),
        "x": (n((K, T)) * s).astype(np.float32),
    }


def reference(w, x):
    w_hi, w_lo = split(w)
    w_hi_, w_lo_ = mxq(w_hi, 0, "e4m3"), mxq(w_lo, 0, "e4m3")
    x_hi, x_lo = split(x)
    x_hi_, x_lo_ = mxq(x_hi, 0, "e4m3"), mxq(x_lo, 0, "e4m3")
    y = x_hi_.T @ w_hi_ + x_lo_.T @ w_hi_ + x_hi_.T @ w_lo_
    return y

@@ -1,0 +1,172 @@
+from contextlib import ExitStack
+
+import concourse.mybir as mybir
+
+K, N, T = 1536, 1536, 512
+FLOPS = 3 * 2 * K * N * T
+
+F32 = mybir.dt.float32
+BF16 = mybir.dt.bfloat16
+I32 = mybir.dt.int32
+U32 = mybir.dt.uint32
+U8 = mybir.dt.uint8
+FP8X4 = mybir.dt.float8_e4m3fn_x4
+ALU = mybir.AluOpType
+
+P = 128
+PACK = 4
+K_PASS = P * PACK
+PASSES = K // K_PASS
+T_TILES = T // P
+RUN = 4
+HI_MASK = -983056
+
+
+def tile_mix_split3_tm_none_kernel(tc, w, x, out):
+    nc = tc.nc
+
+    n_groups = [(0, 512), (512, 512), (1024, 256), (1280, 256)]
+    x_cuts = [[(0, 64), (64, 64), (128, 128), (256, 256)], [(0, 512)], [(0, 512)]]
+    units = []
+    for c in range(PASSES):
+        for (a, width) in x_cuts[c]:
+            units.append(("x", c, a, width, 0))
+        units.append(("w", c, n_groups[0][0], n_groups[0][1], 0))
+    for g in range(1, len(n_groups)):
+        for c in range(PASSES):
+            a, width = n_groups[g]
+            units.append(("w", c, a, width, g))
+    last = len(units) - 1
+
+    with ExitStack() as ctx:
+        keep = ctx.enter_context(tc.tile_pool(name="keep", bufs=1))
+        his = ctx.enter_context(tc.tile_pool(name="his", bufs=4))
+        los = ctx.enter_context(tc.tile_pool(name="los", bufs=3))
+        outs = ctx.enter_context(tc.tile_pool(name="outs", bufs=6))
+        psum = ctx.enter_context(tc.psum_pool(name="psum", bufs=2))
+        ctx.enter_context(tc.manual_schedule())
+
+        raw = []
+        codes = []
+        x_codes = []
+        for c in range(PASSES):
+            x_codes.append([
+                keep.tile([P, T], U32, name="xhc%d" % c, align_bytes=64),
+                keep.tile([P, T], U8, name="xhs%d" % c, align_bytes=64),
+                keep.tile([P, T], U32, name="xlc%d" % c, align_bytes=64),
+                keep.tile([P, T], U8, name="xls%d" % c, align_bytes=64),
+            ])
+        for u, (operand, c, a, width, g) in enumerate(units):
+            r = keep.tile([P, PACK, width], F32, name="raw%d" % u, align_bytes=64)
+            src = x if operand == "x" else w
+            nc.sync.dma_start(
+                out=r[:],
+                in_=src[c * K_PASS:(c + 1) * K_PASS, a:a + width].rearrange("(p j) n -> p j n", j=PACK),
+            )
+            raw.append(r)
+            if operand == "x":
+                codes.append([t[:, a:a + width] for t in x_codes[c]])
+            else:
+                hc = keep.tile([P, width], U32, name="whc%d" % u, align_bytes=64)
+                hs = keep.tile([P, width], U8, name="whs%d" % u, align_bytes=64)
+                lc = keep.tile([P, width], U32, name="wlc%d" % u, align_bytes=64)
+                ls = keep.tile([P, width], U8, name="wls%d" % u, align_bytes=64)
+                codes.append([hc[:], hs[:], lc[:], ls[:]])
+
+        hi = {}
+        lo = {}
+        acc = {}
+
+        def grouped(t):
+            return t.rearrange("p (c i j) -> p c j i", i=RUN, j=PACK)
+
+        def top_halves(u):
+            width = units[u][3]
+            h = his.tile([P, PACK * width], BF16, name="h", align_bytes=64)
+            halves = raw[u][:].rearrange("p j n -> p (j n)").bitcast(BF16)
+            copy = nc.vector.tensor_copy if u == 0 else nc.scalar.copy
+            copy(
+                out=grouped(h[:]),
+                in_=halves.rearrange("p (j c i e) -> p c j i e", j=PACK, i=RUN, e=2)[:, :, :, :, 1],
+            )
+            hi[u] = h
+
+        def mask(u):
+            words = hi[u][:].bitcast(I32)
+            nc.vector.tensor_scalar(out=words, in0=words, scalar1=HI_MASK, scalar2=None, op0=ALU.bitwise_and)
+
+        def subtract(u, pieces=1):
+            width = units[u][3]
+            lo[u] = los.tile([P, PACK * width], BF16, name="l", align_bytes=64)
+            step = width // pieces
+            for a in range(0, width, step):
+                cols = slice(PACK * a, PACK * (a + step))
+                nc.vector.tensor_tensor(
+                    out=grouped(lo[u][:, cols]),
+                    in0=raw[u][:, :, a:a + step].rearrange("p j (c i) -> p c j i", i=RUN),
+                    in1=grouped(hi[u][:, cols]),
+                    op=ALU.subtract,
+                )
+
+        def quantize(u, values, part, pieces=1):
+            width = units[u][3]
+            step = width // pieces
+            for a in range(0, width, step):
+                nc.vector.quantize_mx(
+                    out=codes[u][part][:, a:a + step].bitcast(FP8X4),
+                    scales=codes[u][part + 1][:, a:a + step],
+                    in_=values[u][:, PACK * a:PACK * (a + step)],
+                )
+
+        def multiply(u, part):
+            operand, c, a, width, g = units[u]
+            if operand == "x":
+                return
+            xc = x_codes[c]
+            for t in range(T_TILES):
+                if c == 0 and part == 0:
+                    acc[g, t] = psum.tile([P, width], F32, name="acc%d" % t)
+                first = a - n_groups[g][0]
+                cols = slice(t * P, (t + 1) * P)
+                for xp in ((0, 2) if part == 0 else (0,)):
+                    nc.tensor.matmul_mx(
+                        out=acc[g, t][:, first:first + width],
+                        lhsT=xc[xp][:, cols].bitcast(FP8X4),
+                        lhsT_scale=xc[xp + 1][:, cols],
+                        rhs=codes[u][part].bitcast(FP8X4),
+                        rhs_scale=codes[u][part + 1],
+                        start=(c == 0 and part == 0 and xp == 0),
+                        stop=(c == PASSES - 1 and part == 2),
+                    )
+
+        def drain(g, first, width):
+            a = n_groups[g][0] + first
+            for t in range(T_TILES):
+                o = outs.tile([P, width], F32, name="o", align_bytes=64)
+                if g == len(n_groups) - 1 and t % 2 == 1:
+                    nc.vector.tensor_copy(out=o[:], in_=acc[g, t][:, first:first + width])
+                else:
+                    nc.scalar.copy(out=o[:], in_=acc[g, t][:, first:first + width])
+                nc.sync.dma_start(out=out[t * P:(t + 1) * P, a:a + width], in_=o[:])
+
+        for u in range(3):
+            top_halves(u)
+        mask(0)
+        quantize(0, hi, 0)
+        multiply(0, 0)
+        for u in range(last + 1):
+            if u + 3 <= last:
+                top_halves(u + 3)
+            pieces = 2 if u == last else 1
+            subtract(u, pieces)
+            if u < last:
+                mask(u + 1)
+            quantize(u, lo, 2, pieces)
+            if u < last:
+                quantize(u + 1, hi, 0)
+            multiply(u, 2)
+            if u < last:
+                multiply(u + 1, 0)
+            operand, c, a, width, g = units[u]
+            if operand == "w" and c == PASSES - 1:
+                drain(g, a - n_groups[g][0], width)

@@ -19,6 +19,7 @@ K_PASS = P * PACK
 PASSES = K // K_PASS
 T_TILES = T // P
 RUN = 4
+SUB_RUN = 2
 HI_MASK = -983056
 
 
@@ -77,8 +78,8 @@ def tile_mix_split3_tm_none_kernel(tc, w, x, out):
         lo = {}
         acc = {}
 
-        def grouped(t):
-            return t.rearrange("p (c i j) -> p c j i", i=RUN, j=PACK)
+        def grouped(t, run):
+            return t.rearrange("p (c i j) -> p c j i", i=run, j=PACK)
 
         def top_halves(u):
             width = units[u][3]
@@ -86,7 +87,7 @@ def tile_mix_split3_tm_none_kernel(tc, w, x, out):
             halves = raw[u][:].rearrange("p j n -> p (j n)").bitcast(BF16)
             copy = nc.vector.tensor_copy if u == 0 else nc.scalar.copy
             copy(
-                out=grouped(h[:]),
+                out=grouped(h[:], RUN),
                 in_=halves.rearrange("p (j c i e) -> p c j i e", j=PACK, i=RUN, e=2)[:, :, :, :, 1],
             )
             hi[u] = h
@@ -102,9 +103,9 @@ def tile_mix_split3_tm_none_kernel(tc, w, x, out):
             for a in range(0, width, step):
                 cols = slice(PACK * a, PACK * (a + step))
                 nc.vector.tensor_tensor(
-                    out=grouped(lo[u][:, cols]),
-                    in0=raw[u][:, :, a:a + step].rearrange("p j (c i) -> p c j i", i=RUN),
-                    in1=grouped(hi[u][:, cols]),
+                    out=grouped(lo[u][:, cols], SUB_RUN),
+                    in0=raw[u][:, :, a:a + step].rearrange("p j (c i) -> p c j i", i=SUB_RUN),
+                    in1=grouped(hi[u][:, cols], SUB_RUN),
                     op=ALU.subtract,
                 )
 

@@ -18,156 +18,212 @@ PACK = 4
 K_PASS = P * PACK
 PASSES = K // K_PASS
 T_TILES = T // P
-RUN = 4
+COPY_RUN = 4
 SUB_RUN = 2
 HI_MASK = -983056
+
+N_GROUPS = [(0, 512), (512, 512), (1024, 256), (1280, 256)]
+
+
+def wb(g, c, pieces=1):
+    return ("w", c, N_GROUPS[g][0], [N_GROUPS[g][1] // pieces] * pieces, g)
+
+
+BATCHES = [
+    [("x", 0, 0, [64, 64, 128, 128, 128], 0)],
+    [wb(0, 0, 2)],
+    [("x", 1, 0, [512], 0)],
+    [wb(0, 1)],
+    [("x", 2, 0, [512], 0)],
+    [wb(0, 2), wb(1, 0)],
+    [wb(1, 1), wb(1, 2)],
+    [wb(2, 0), wb(2, 1)],
+    [wb(2, 2), wb(3, 0), wb(3, 1), wb(3, 2, 2)],
+]
 
 
 def tile_mix_split3_tm_none_kernel(tc, w, x, out):
     nc = tc.nc
-
-    n_groups = [(0, 512), (512, 512), (1024, 256), (1280, 256)]
-    x_cuts = [[(0, 64), (64, 64), (128, 128), (256, 256)], [(0, 512)], [(0, 512)]]
-    units = []
-    for c in range(PASSES):
-        for (a, width) in x_cuts[c]:
-            units.append(("x", c, a, width, 0))
-        units.append(("w", c, n_groups[0][0], n_groups[0][1], 0))
-    for g in range(1, len(n_groups)):
-        for c in range(PASSES):
-            a, width = n_groups[g]
-            units.append(("w", c, a, width, g))
-    last = len(units) - 1
+    last = len(BATCHES) - 1
 
     with ExitStack() as ctx:
         keep = ctx.enter_context(tc.tile_pool(name="keep", bufs=1))
-        his = ctx.enter_context(tc.tile_pool(name="his", bufs=4))
-        los = ctx.enter_context(tc.tile_pool(name="los", bufs=3))
+        his = ctx.enter_context(tc.tile_pool(name="his", bufs=3))
+        los = ctx.enter_context(tc.tile_pool(name="los", bufs=2))
         outs = ctx.enter_context(tc.tile_pool(name="outs", bufs=6))
         psum = ctx.enter_context(tc.psum_pool(name="psum", bufs=2))
         ctx.enter_context(tc.manual_schedule())
 
-        raw = []
         codes = []
-        x_codes = []
-        for c in range(PASSES):
-            x_codes.append([
-                keep.tile([P, T], U32, name="xhc%d" % c, align_bytes=64),
-                keep.tile([P, T], U8, name="xhs%d" % c, align_bytes=64),
-                keep.tile([P, T], U32, name="xlc%d" % c, align_bytes=64),
-                keep.tile([P, T], U8, name="xls%d" % c, align_bytes=64),
+        pieces = []
+        blocks = []
+        x_at = {}
+        for b, batch in enumerate(BATCHES):
+            width = sum(sum(block[3]) for block in batch)
+            codes.append([
+                keep.tile([P, width], U32, name="hc%d" % b, align_bytes=64),
+                keep.tile([P, width], U8, name="hs%d" % b, align_bytes=64),
+                keep.tile([P, width], U32, name="lc%d" % b, align_bytes=64),
+                keep.tile([P, width], U8, name="ls%d" % b, align_bytes=64),
             ])
-        for u, (operand, c, a, width, g) in enumerate(units):
-            r = keep.tile([P, PACK, width], F32, name="raw%d" % u, align_bytes=64)
-            src = x if operand == "x" else w
-            nc.sync.dma_start(
-                out=r[:],
-                in_=src[c * K_PASS:(c + 1) * K_PASS, a:a + width].rearrange("(p j) n -> p j n", j=PACK),
-            )
-            raw.append(r)
-            if operand == "x":
-                codes.append([t[:, a:a + width] for t in x_codes[c]])
-            else:
-                hc = keep.tile([P, width], U32, name="whc%d" % u, align_bytes=64)
-                hs = keep.tile([P, width], U8, name="whs%d" % u, align_bytes=64)
-                lc = keep.tile([P, width], U32, name="wlc%d" % u, align_bytes=64)
-                ls = keep.tile([P, width], U8, name="wls%d" % u, align_bytes=64)
-                codes.append([hc[:], hs[:], lc[:], ls[:]])
+            batch_pieces = []
+            batch_blocks = []
+            at = 0
+            for i, (operand, c, a, widths, g) in enumerate(batch):
+                if operand == "x":
+                    x_at[c] = (b, at)
+                else:
+                    batch_blocks.append((at, c, g))
+                src = x if operand == "x" else w
+                for j, wd in enumerate(widths):
+                    raw = keep.tile([P, PACK, wd], F32, name="raw%d_%d_%d" % (b, i, j), align_bytes=64)
+                    nc.sync.dma_start(
+                        out=raw[:],
+                        in_=src[c * K_PASS:(c + 1) * K_PASS, a:a + wd].rearrange("(p j) n -> p j n", j=PACK),
+                    )
+                    batch_pieces.append((raw, at, wd))
+                    a += wd
+                    at += wd
+            pieces.append(batch_pieces)
+            blocks.append(batch_blocks)
 
         hi = {}
         lo = {}
         acc = {}
 
+        def width_of(b):
+            return sum(p[2] for p in pieces[b])
+
         def grouped(t, run):
             return t.rearrange("p (c i j) -> p c j i", i=run, j=PACK)
 
-        def top_halves(u):
-            width = units[u][3]
-            h = his.tile([P, PACK * width], BF16, name="h", align_bytes=64)
-            halves = raw[u][:].rearrange("p j n -> p (j n)").bitcast(BF16)
-            copy = nc.vector.tensor_copy if u == 0 else nc.scalar.copy
-            copy(
-                out=grouped(h[:], RUN),
-                in_=halves.rearrange("p (j c i e) -> p c j i e", j=PACK, i=RUN, e=2)[:, :, :, :, 1],
-            )
-            hi[u] = h
+        def open_hi(b):
+            hi[b] = his.tile([P, PACK * width_of(b)], BF16, name="h", align_bytes=64)
 
-        def mask(u):
-            words = hi[u][:].bitcast(I32)
+        def open_lo(b):
+            lo[b] = los.tile([P, PACK * width_of(b)], BF16, name="l", align_bytes=64)
+
+        def top_halves(b, i, copy):
+            raw, at, wd = pieces[b][i]
+            halves = raw[:].rearrange("p j n -> p (j n)").bitcast(BF16)
+            copy(
+                out=grouped(hi[b][:, PACK * at:PACK * (at + wd)], COPY_RUN),
+                in_=halves.rearrange("p (j c i e) -> p c j i e", j=PACK, i=COPY_RUN, e=2)[:, :, :, :, 1],
+            )
+
+        def all_top_halves(b):
+            open_hi(b)
+            for i in range(len(pieces[b])):
+                top_halves(b, i, nc.scalar.copy)
+
+        def mask(b, at, wd):
+            words = hi[b][:, PACK * at:PACK * (at + wd)].bitcast(I32)
             nc.vector.tensor_scalar(out=words, in0=words, scalar1=HI_MASK, scalar2=None, op0=ALU.bitwise_and)
 
-        def subtract(u, pieces=1):
-            width = units[u][3]
-            lo[u] = los.tile([P, PACK * width], BF16, name="l", align_bytes=64)
-            step = width // pieces
-            for a in range(0, width, step):
-                cols = slice(PACK * a, PACK * (a + step))
-                nc.vector.tensor_tensor(
-                    out=grouped(lo[u][:, cols], SUB_RUN),
-                    in0=raw[u][:, :, a:a + step].rearrange("p j (c i) -> p c j i", i=SUB_RUN),
-                    in1=grouped(hi[u][:, cols], SUB_RUN),
-                    op=ALU.subtract,
-                )
+        def mask_piece(b, i):
+            mask(b, pieces[b][i][1], pieces[b][i][2])
 
-        def quantize(u, values, part, pieces=1):
-            width = units[u][3]
-            step = width // pieces
-            for a in range(0, width, step):
-                nc.vector.quantize_mx(
-                    out=codes[u][part][:, a:a + step].bitcast(FP8X4),
-                    scales=codes[u][part + 1][:, a:a + step],
-                    in_=values[u][:, PACK * a:PACK * (a + step)],
-                )
+        def subtract(b, i):
+            raw, at, wd = pieces[b][i]
+            cols = slice(PACK * at, PACK * (at + wd))
+            nc.vector.tensor_tensor(
+                out=grouped(lo[b][:, cols], SUB_RUN),
+                in0=raw[:].rearrange("p j (c i) -> p c j i", i=SUB_RUN),
+                in1=grouped(hi[b][:, cols], SUB_RUN),
+                op=ALU.subtract,
+            )
 
-        def multiply(u, part):
-            operand, c, a, width, g = units[u]
-            if operand == "x":
-                return
-            xc = x_codes[c]
+        def quantize(b, values, part, at, wd):
+            nc.vector.quantize_mx(
+                out=codes[b][part][:, at:at + wd].bitcast(FP8X4),
+                scales=codes[b][part + 1][:, at:at + wd],
+                in_=values[b][:, PACK * at:PACK * (at + wd)],
+            )
+
+        def multiply(b, block, part):
+            at, c, g = block
+            wd = N_GROUPS[g][1]
+            xb, x0 = x_at[c]
             for t in range(T_TILES):
                 if c == 0 and part == 0:
-                    acc[g, t] = psum.tile([P, width], F32, name="acc%d" % t)
-                first = a - n_groups[g][0]
-                cols = slice(t * P, (t + 1) * P)
+                    acc[g, t] = psum.tile([P, wd], F32, name="acc%d" % t)
+                rows = slice(x0 + t * P, x0 + (t + 1) * P)
                 for xp in ((0, 2) if part == 0 else (0,)):
                     nc.tensor.matmul_mx(
-                        out=acc[g, t][:, first:first + width],
-                        lhsT=xc[xp][:, cols].bitcast(FP8X4),
-                        lhsT_scale=xc[xp + 1][:, cols],
-                        rhs=codes[u][part].bitcast(FP8X4),
-                        rhs_scale=codes[u][part + 1],
+                        out=acc[g, t][:],
+                        lhsT=codes[xb][xp][:, rows].bitcast(FP8X4),
+                        lhsT_scale=codes[xb][xp + 1][:, rows],
+                        rhs=codes[b][part][:, at:at + wd].bitcast(FP8X4),
+                        rhs_scale=codes[b][part + 1][:, at:at + wd],
                         start=(c == 0 and part == 0 and xp == 0),
                         stop=(c == PASSES - 1 and part == 2),
                     )
 
-        def drain(g, first, width):
-            a = n_groups[g][0] + first
-            for t in range(T_TILES):
-                o = outs.tile([P, width], F32, name="o", align_bytes=64)
-                if g == len(n_groups) - 1 and t % 2 == 1:
-                    nc.vector.tensor_copy(out=o[:], in_=acc[g, t][:, first:first + width])
-                else:
-                    nc.scalar.copy(out=o[:], in_=acc[g, t][:, first:first + width])
-                nc.sync.dma_start(out=out[t * P:(t + 1) * P, a:a + width], in_=o[:])
+        def multiply_hi(b):
+            for block in blocks[b]:
+                multiply(b, block, 0)
 
-        for u in range(3):
-            top_halves(u)
-        mask(0)
-        quantize(0, hi, 0)
-        multiply(0, 0)
-        for u in range(last + 1):
-            if u + 3 <= last:
-                top_halves(u + 3)
-            pieces = 2 if u == last else 1
-            subtract(u, pieces)
-            if u < last:
-                mask(u + 1)
-            quantize(u, lo, 2, pieces)
-            if u < last:
-                quantize(u + 1, hi, 0)
-            multiply(u, 2)
-            if u < last:
-                multiply(u + 1, 0)
-            operand, c, a, width, g = units[u]
-            if operand == "w" and c == PASSES - 1:
-                drain(g, a - n_groups[g][0], width)
+        def multiply_lo(b, i):
+            block = blocks[b][i]
+            multiply(b, block, 2)
+            if block[1] == PASSES - 1:
+                drain(block[2])
+
+        def drain(g):
+            a, wd = N_GROUPS[g]
+            for t in range(T_TILES):
+                o = outs.tile([P, wd], F32, name="o", align_bytes=64)
+                if g == len(N_GROUPS) - 1 and t % 2 == 1:
+                    nc.vector.tensor_copy(out=o[:], in_=acc[g, t][:])
+                else:
+                    nc.scalar.copy(out=o[:], in_=acc[g, t][:])
+                nc.sync.dma_start(out=out[t * P:(t + 1) * P, a:a + wd], in_=o[:])
+
+        open_hi(0)
+        open_lo(0)
+        n0 = len(pieces[0])
+        top_halves(0, 0, nc.vector.tensor_copy)
+        for i in range(1, n0):
+            top_halves(0, i, nc.scalar.copy)
+        all_top_halves(1)
+        mask_piece(0, 0)
+        for i in range(1, n0):
+            mask_piece(0, i)
+            subtract(0, i - 1)
+        quantize(0, hi, 0, 0, width_of(0))
+        subtract(0, n0 - 1)
+        mask_piece(1, 0)
+        quantize(0, lo, 2, 0, width_of(0))
+        mask_piece(1, 1)
+        all_top_halves(2)
+        open_lo(1)
+        subtract(1, 0)
+        quantize(1, hi, 0, 0, width_of(1))
+        multiply_hi(1)
+
+        for b in range(1, last):
+            if b + 2 <= last:
+                all_top_halves(b + 2)
+            if b > 1:
+                open_lo(b)
+            for i in range(1 if b == 1 else 0, len(pieces[b])):
+                subtract(b, i)
+            mask(b + 1, 0, width_of(b + 1))
+            quantize(b, lo, 2, 0, width_of(b))
+            quantize(b + 1, hi, 0, 0, width_of(b + 1))
+            for i in range(len(blocks[b])):
+                multiply_lo(b, i)
+            multiply_hi(b + 1)
+
+        open_lo(last)
+        n_last = len(pieces[last])
+        n_blocks = len(blocks[last])
+        for i in range(n_last + 1):
+            if i < n_last:
+                subtract(last, i)
+            if i > 0:
+                raw, at, wd = pieces[last][i - 1]
+                quantize(last, lo, 2, at, wd)
+                if i < n_blocks:
+                    multiply_lo(last, i - 1)
+        multiply_lo(last, n_blocks - 1)

@@ -22,6 +22,8 @@ COPY_RUN = 4
 SUB_RUN = 2
 HI_MASK = -983056
 
+FINE = 3
+
 N_GROUPS = [(0, 512), (512, 512), (1024, 256), (1280, 256)]
 
 
@@ -30,15 +32,18 @@ def wb(g, c, pieces=1):
 
 
 BATCHES = [
-    [("x", 0, 0, [64, 64, 128, 128, 128], 0)],
+    [("x", 0, 0, [128, 128, 128, 128], 0)],
     [wb(0, 0, 2)],
-    [("x", 1, 0, [512], 0)],
+    [("x", 1, 0, [256, 256], 0)],
     [wb(0, 1)],
     [("x", 2, 0, [512], 0)],
     [wb(0, 2), wb(1, 0)],
-    [wb(1, 1), wb(1, 2)],
+    [wb(1, 1)],
+    [wb(1, 2)],
     [wb(2, 0), wb(2, 1)],
-    [wb(2, 2), wb(3, 0), wb(3, 1), wb(3, 2, 2)],
+    [wb(2, 2), wb(3, 0)],
+    [wb(3, 1)],
+    [wb(3, 2, 2)],
 ]
 
 
@@ -50,7 +55,7 @@ def tile_mix_split3_tm_none_kernel(tc, w, x, out):
         keep = ctx.enter_context(tc.tile_pool(name="keep", bufs=1))
         his = ctx.enter_context(tc.tile_pool(name="his", bufs=3))
         los = ctx.enter_context(tc.tile_pool(name="los", bufs=2))
-        outs = ctx.enter_context(tc.tile_pool(name="outs", bufs=6))
+        outs = ctx.enter_context(tc.tile_pool(name="outs", bufs=10))
         psum = ctx.enter_context(tc.psum_pool(name="psum", bufs=2))
         ctx.enter_context(tc.manual_schedule())
 
@@ -120,9 +125,6 @@ def tile_mix_split3_tm_none_kernel(tc, w, x, out):
             words = hi[b][:, PACK * at:PACK * (at + wd)].bitcast(I32)
             nc.vector.tensor_scalar(out=words, in0=words, scalar1=HI_MASK, scalar2=None, op0=ALU.bitwise_and)
 
-        def mask_piece(b, i):
-            mask(b, pieces[b][i][1], pieces[b][i][2])
-
         def subtract(b, i):
             raw, at, wd = pieces[b][i]
             cols = slice(PACK * at, PACK * (at + wd))
@@ -179,41 +181,53 @@ def tile_mix_split3_tm_none_kernel(tc, w, x, out):
                     nc.scalar.copy(out=o[:], in_=acc[g, t][:])
                 nc.sync.dma_start(out=out[t * P:(t + 1) * P, a:a + wd], in_=o[:])
 
+        steps = []
+        for b in range(last + 1):
+            n = len(pieces[b])
+            if b < FINE:
+                for i in range(n):
+                    steps.append((b, [i], i == n - 1))
+            else:
+                steps.append((b, list(range(n)), True))
+
+        def mask_step(step):
+            b, members, ends = step
+            a = pieces[b][members[0]][1]
+            e = pieces[b][members[-1]][1] + pieces[b][members[-1]][2]
+            mask(b, a, e - a)
+
+        def subtract_step(step):
+            for i in step[1]:
+                subtract(step[0], i)
+
         open_hi(0)
-        open_lo(0)
-        n0 = len(pieces[0])
         top_halves(0, 0, nc.vector.tensor_copy)
-        for i in range(1, n0):
+        for i in range(1, len(pieces[0])):
             top_halves(0, i, nc.scalar.copy)
         all_top_halves(1)
-        mask_piece(0, 0)
-        for i in range(1, n0):
-            mask_piece(0, i)
-            subtract(0, i - 1)
-        quantize(0, hi, 0, 0, width_of(0))
-        subtract(0, n0 - 1)
-        mask_piece(1, 0)
-        quantize(0, lo, 2, 0, width_of(0))
-        mask_piece(1, 1)
-        all_top_halves(2)
-        open_lo(1)
-        subtract(1, 0)
-        quantize(1, hi, 0, 0, width_of(1))
-        multiply_hi(1)
-
-        for b in range(1, last):
-            if b + 2 <= last:
-                all_top_halves(b + 2)
-            if b > 1:
+        mask_step(steps[0])
+        for k, step in enumerate(steps[:-1]):
+            b, members, ends = step
+            after = steps[k + 1]
+            if members[0] == 0:
                 open_lo(b)
-            for i in range(1 if b == 1 else 0, len(pieces[b])):
-                subtract(b, i)
-            mask(b + 1, 0, width_of(b + 1))
-            quantize(b, lo, 2, 0, width_of(b))
-            quantize(b + 1, hi, 0, 0, width_of(b + 1))
-            for i in range(len(blocks[b])):
-                multiply_lo(b, i)
-            multiply_hi(b + 1)
+                if b + 2 <= last:
+                    all_top_halves(b + 2)
+            mask_first = b != 1 and not ends
+            if mask_first:
+                mask_step(after)
+            subtract_step(step)
+            if not mask_first:
+                mask_step(after)
+            if ends:
+                quantize(b, lo, 2, 0, width_of(b))
+            if after[2]:
+                quantize(after[0], hi, 0, 0, width_of(after[0]))
+            if ends:
+                for i in range(len(blocks[b])):
+                    multiply_lo(b, i)
+            if after[2]:
+                multiply_hi(after[0])
 
         open_lo(last)
         n_last = len(pieces[last])

from contextlib import ExitStack

import concourse.mybir as mybir

K, N, T = 1536, 1536, 512
FLOPS = 3 * 2 * K * N * T

F32 = mybir.dt.float32
BF16 = mybir.dt.bfloat16
I32 = mybir.dt.int32
U32 = mybir.dt.uint32
U8 = mybir.dt.uint8
FP8X4 = mybir.dt.float8_e4m3fn_x4
ALU = mybir.AluOpType

P = 128
PACK = 4
K_PASS = P * PACK
PASSES = K // K_PASS
T_TILES = T // P
COPY_RUN = 4
SUB_RUN = 2
HI_MASK = -983056

FINE = 3

N_GROUPS = [(0, 512), (512, 512), (1024, 256), (1280, 256)]


def wb(g, c, pieces=1):
    return ("w", c, N_GROUPS[g][0], [N_GROUPS[g][1] // pieces] * pieces, g)


BATCHES = [
    [("x", 0, 0, [128, 128, 128, 128], 0)],
    [wb(0, 0, 2)],
    [("x", 1, 0, [256, 256], 0)],
    [wb(0, 1)],
    [("x", 2, 0, [512], 0)],
    [wb(0, 2), wb(1, 0)],
    [wb(1, 1)],
    [wb(1, 2)],
    [wb(2, 0), wb(2, 1)],
    [wb(2, 2), wb(3, 0)],
    [wb(3, 1)],
    [wb(3, 2, 2)],
]


def tile_mix_split3_tm_none_kernel(tc, w, x, out):
    nc = tc.nc
    last = len(BATCHES) - 1

    with ExitStack() as ctx:
        keep = ctx.enter_context(tc.tile_pool(name="keep", bufs=1))
        his = ctx.enter_context(tc.tile_pool(name="his", bufs=3))
        los = ctx.enter_context(tc.tile_pool(name="los", bufs=2))
        outs = ctx.enter_context(tc.tile_pool(name="outs", bufs=10))
        psum = ctx.enter_context(tc.psum_pool(name="psum", bufs=2))
        ctx.enter_context(tc.manual_schedule())

        codes = []
        pieces = []
        blocks = []
        x_at = {}
        for b, batch in enumerate(BATCHES):
            width = sum(sum(block[3]) for block in batch)
            codes.append([
                keep.tile([P, width], U32, name="hc%d" % b, align_bytes=64),
                keep.tile([P, width], U8, name="hs%d" % b, align_bytes=64),
                keep.tile([P, width], U32, name="lc%d" % b, align_bytes=64),
                keep.tile([P, width], U8, name="ls%d" % b, align_bytes=64),
            ])
            batch_pieces = []
            batch_blocks = []
            at = 0
            for i, (operand, c, a, widths, g) in enumerate(batch):
                if operand == "x":
                    x_at[c] = (b, at)
                else:
                    batch_blocks.append((at, c, g))
                src = x if operand == "x" else w
                for j, wd in enumerate(widths):
                    raw = keep.tile([P, PACK, wd], F32, name="raw%d_%d_%d" % (b, i, j), align_bytes=64)
                    nc.sync.dma_start(
                        out=raw[:],
                        in_=src[c * K_PASS:(c + 1) * K_PASS, a:a + wd].rearrange("(p j) n -> p j n", j=PACK),
                    )
                    batch_pieces.append((raw, at, wd))
                    a += wd
                    at += wd
            pieces.append(batch_pieces)
            blocks.append(batch_blocks)

        hi = {}
        lo = {}
        acc = {}

        def width_of(b):
            return sum(p[2] for p in pieces[b])

        def grouped(t, run):
            return t.rearrange("p (c i j) -> p c j i", i=run, j=PACK)

        def open_hi(b):
            hi[b] = his.tile([P, PACK * width_of(b)], BF16, name="h", align_bytes=64)

        def open_lo(b):
            lo[b] = los.tile([P, PACK * width_of(b)], BF16, name="l", align_bytes=64)

        def top_halves(b, i, copy):
            raw, at, wd = pieces[b][i]
            halves = raw[:].rearrange("p j n -> p (j n)").bitcast(BF16)
            copy(
                out=grouped(hi[b][:, PACK * at:PACK * (at + wd)], COPY_RUN),
                in_=halves.rearrange("p (j c i e) -> p c j i e", j=PACK, i=COPY_RUN, e=2)[:, :, :, :, 1],
            )

        def all_top_halves(b):
            open_hi(b)
            for i in range(len(pieces[b])):
                top_halves(b, i, nc.scalar.copy)

        def mask(b, at, wd):
            words = hi[b][:, PACK * at:PACK * (at + wd)].bitcast(I32)
            nc.vector.tensor_scalar(out=words, in0=words, scalar1=HI_MASK, scalar2=None, op0=ALU.bitwise_and)

        def subtract(b, i):
            raw, at, wd = pieces[b][i]
            cols = slice(PACK * at, PACK * (at + wd))
            nc.vector.tensor_tensor(
                out=grouped(lo[b][:, cols], SUB_RUN),
                in0=raw[:].rearrange("p j (c i) -> p c j i", i=SUB_RUN),
                in1=grouped(hi[b][:, cols], SUB_RUN),
                op=ALU.subtract,
            )

        def quantize(b, values, part, at, wd):
            nc.vector.quantize_mx(
                out=codes[b][part][:, at:at + wd].bitcast(FP8X4),
                scales=codes[b][part + 1][:, at:at + wd],
                in_=values[b][:, PACK * at:PACK * (at + wd)],
            )

        def multiply(b, block, part):
            at, c, g = block
            wd = N_GROUPS[g][1]
            xb, x0 = x_at[c]
            for t in range(T_TILES):
                if c == 0 and part == 0:
                    acc[g, t] = psum.tile([P, wd], F32, name="acc%d" % t)
                rows = slice(x0 + t * P, x0 + (t + 1) * P)
                for xp in ((0, 2) if part == 0 else (0,)):
                    nc.tensor.matmul_mx(
                        out=acc[g, t][:],
                        lhsT=codes[xb][xp][:, rows].bitcast(FP8X4),
                        lhsT_scale=codes[xb][xp + 1][:, rows],
                        rhs=codes[b][part][:, at:at + wd].bitcast(FP8X4),
                        rhs_scale=codes[b][part + 1][:, at:at + wd],
                        start=(c == 0 and part == 0 and xp == 0),
                        stop=(c == PASSES - 1 and part == 2),
                    )

        def multiply_hi(b):
            for block in blocks[b]:
                multiply(b, block, 0)

        def multiply_lo(b, i):
            block = blocks[b][i]
            multiply(b, block, 2)
            if block[1] == PASSES - 1:
                drain(block[2])

        def drain(g):
            a, wd = N_GROUPS[g]
            for t in range(T_TILES):
                o = outs.tile([P, wd], F32, name="o", align_bytes=64)
                if g == len(N_GROUPS) - 1 and t % 2 == 1:
                    nc.vector.tensor_copy(out=o[:], in_=acc[g, t][:])
                else:
                    nc.scalar.copy(out=o[:], in_=acc[g, t][:])
                nc.sync.dma_start(out=out[t * P:(t + 1) * P, a:a + wd], in_=o[:])

        steps = []
        for b in range(last + 1):
            n = len(pieces[b])
            if b < FINE:
                for i in range(n):
                    steps.append((b, [i], i == n - 1))
            else:
                steps.append((b, list(range(n)), True))

        def mask_step(step):
            b, members, ends = step
            a = pieces[b][members[0]][1]
            e = pieces[b][members[-1]][1] + pieces[b][members[-1]][2]
            mask(b, a, e - a)

        def subtract_step(step):
            for i in step[1]:
                subtract(step[0], i)

        open_hi(0)
        top_halves(0, 0, nc.vector.tensor_copy)
        for i in range(1, len(pieces[0])):
            top_halves(0, i, nc.scalar.copy)
        all_top_halves(1)
        mask_step(steps[0])
        for k, step in enumerate(steps[:-1]):
            b, members, ends = step
            after = steps[k + 1]
            if members[0] == 0:
                open_lo(b)
                if b + 2 <= last:
                    all_top_halves(b + 2)
            mask_first = b != 1 and not ends
            if mask_first:
                mask_step(after)
            subtract_step(step)
            if not mask_first:
                mask_step(after)
            if ends:
                quantize(b, lo, 2, 0, width_of(b))
            if after[2]:
                quantize(after[0], hi, 0, 0, width_of(after[0]))
            if ends:
                for i in range(len(blocks[b])):
                    multiply_lo(b, i)
            if after[2]:
                multiply_hi(after[0])

        open_lo(last)
        n_last = len(pieces[last])
        n_blocks = len(blocks[last])
        for i in range(n_last + 1):
            if i < n_last:
                subtract(last, i)
            if i > 0:
                raw, at, wd = pieces[last][i - 1]
                quantize(last, lo, 2, at, wd)
                if i < n_blocks:
                    multiply_lo(last, i - 1)
        multiply_lo(last, n_blocks - 1)
